import numpy as np
import ml_dtypes


def mxq(x, axis, fmt="e4m3"):
    dtype, down = {"e4m3": (ml_dtypes.float8_e4m3fn, 7), "e5m2": (ml_dtypes.float8_e5m2, 14)}[fmt]
    v = np.moveaxis(np.asarray(x, np.float32).astype(ml_dtypes.bfloat16).astype(np.float64), axis, -1)
    blocks = v.reshape(v.shape[:-1] + (-1, 32))
    amax = np.abs(blocks).max(-1, keepdims=True)
    byte = np.maximum(np.where(amax > 0, np.frexp(amax)[1] - 1 + 127, 0) - down, 1)
    scale = np.exp2(byte - 127.0)
    codes = (blocks / scale).astype(np.float32).astype(dtype).astype(np.float64)
    return np.moveaxis((codes * scale).reshape(v.shape), -1, axis)


WIDE = False


def mx_kscale(k):
    if not WIDE:
        return np.ones(k)
    levels = np.array([10, -10, 5, -5, 0])
    if k % 512:
        return np.exp2(np.random.permutation(np.resize(levels, k // 32))).repeat(32)
    a = np.empty((k // 512, 16))
    for p in range(k // 512):
        a[p, :8] = np.random.permutation(np.resize(levels, 8))
        for g in range(8):
            far = levels[np.abs(levels - a[p, g]) >= 10]
            a[p, g + 8] = far[np.random.randint(len(far))]
    return np.exp2(a.ravel()).repeat(32)


def f64(x):
    return np.asarray(x).astype(np.float64)


def striped(idx):
    return np.tile(idx.reshape(-1, 16).T, (8, 1)).astype(np.uint16)


def unstriped(offs):
    return offs[:16].T.reshape(-1).astype(np.int64)


E2M1 = np.array([0.0, 0.5, 1.0, 1.5, 2.0, 3.0, 4.0, 6.0, -0.0, -0.5, -1.0, -1.5, -2.0, -3.0, -4.0, -6.0])


def pack_weight(w, fmt):
    k, n = w.shape
    w = f64(np.asarray(w, np.float32).astype(ml_dtypes.bfloat16)).reshape(k // 32, 32, n)
    amax = np.abs(w).max(1)
    if fmt == "e4m3":
        byte = np.frexp(amax)[1] - 1 + 127 - 7
    else:
        mant, ex = np.frexp(amax / 6.0)
        byte = np.where(mant > 0.5, ex, ex - 1) + 127
    byte = np.clip(np.where(amax > 0, byte, 1), 1, 254)
    scaled = (w * np.exp2(127.0 - byte)[:, None, :]).reshape(k, n).astype(np.float32)
    by_word = np.ascontiguousarray(scaled.reshape(k // 512, 128, 4, n).transpose(0, 1, 3, 2))
    if fmt == "e4m3":
        words = by_word.astype(ml_dtypes.float8_e4m3fn).view(np.uint8)
    else:
        c = by_word.astype(ml_dtypes.float4_e2m1fn).view(np.uint8) & 0xF
        words = (c[..., 0::2] | (c[..., 1::2] << 4)).reshape(k // 512, 128, 2 * n)
    return np.ascontiguousarray(words), np.ascontiguousarray(byte.astype(np.uint8).reshape(k // 512, 16, n))


def unpack_weight(words, scales, fmt):
    g, _, n = scales.shape
    words = np.ascontiguousarray(words).reshape(g, 128, n, -1)
    if fmt == "e4m3":
        vals = words.view(ml_dtypes.float8_e4m3fn).astype(np.float64)
    else:
        nib = np.empty((g, 128, n, 4), np.uint8)
        nib[..., 0::2] = words & 0xF
        nib[..., 1::2] = words >> 4
        vals = E2M1[nib]
    vals = vals * np.repeat(np.exp2(scales.astype(np.float64) - 127.0), 8, axis=1)[..., None]
    return vals.transpose(0, 1, 3, 2).reshape(g * 512, n)


def relu(v):
    return np.maximum(v, 0.0)


def d_relu(v):
    return (v > 0).astype(np.float64)


K, T, E, C, H, N = 512, 512, 4, 256, 512, 1536


def by_expert(wq, xq):
    return np.concatenate([wq[e].T @ xq[:, e * C:(e + 1) * C] for e in range(E)], axis=1)


def setup_inputs():
    n = np.random.standard_normal
    s = mx_kscale(N)[:, None]
    u = mx_kscale(H)
    first = np.random.permutation(np.repeat(np.arange(E), T // E))
    second = (first + 1 + np.random.permutation(np.repeat(np.arange(E - 1), -(-T // (E - 1)))[:T])) % E
    while np.bincount(second, minlength=E).max() != T // E:
        load = np.bincount(second, minlength=E); hi, lo = int(load.argmax()), int(load.argmin())
        t = np.flatnonzero((second == hi) & (first != lo))[0]; second[t] = lo
    slot_token = np.empty(E * C, np.int64); pos = np.empty((2, T), np.int64); fill = np.zeros(E, np.int64)
    place = np.stack([np.random.permutation(C) for _ in range(E)])
    for r, deal in enumerate((first, second)):
        for t in np.random.permutation(T):
            e = deal[t]; j = e * C + place[e, fill[e]]; fill[e] += 1; slot_token[j] = t; pos[r, t] = j
    g = np.random.uniform(0.2, 0.8, T)
    w_slot = np.empty(E * C); w_slot[pos[0]] = g; w_slot[pos[1]] = 1.0 - g
    w2 = [pack_weight(m, "e2m1") for m in n((E, N, H)) / np.sqrt(N) / s[None] * u[None, None, :]]
    w1 = [pack_weight(m, "e2m1") for m in n((E, H, K)) / np.sqrt(H) / u[None, :, None]]
    w3 = [pack_weight(m, "e2m1") for m in n((E, H, K)) / np.sqrt(H) / u[None, :, None]]
    return {
        "dyT": (n((N, T)) * s).astype(np.float32),
        "a1": n((H, E * C)).astype(np.float32),
        "a3": n((H, E * C)).astype(np.float32),
        "w2_words": np.stack([m[0] for m in w2]),
        "w2_scales": np.stack([m[1] for m in w2]),
        "w1_words": np.stack([m[0] for m in w1]),
        "w1_scales": np.stack([m[1] for m in w1]),
        "w3_words": np.stack([m[0] for m in w3]),
        "w3_scales": np.stack([m[1] for m in w3]),
        "gate": np.tile(w_slot, (N, 1)).astype(np.float32),
        "offs": striped(slot_token),
        "pos1": striped(pos[0]),
        "pos2": striped(pos[1]),
    }


def reference(dyT, a1, a3, w2_words, w2_scales, w1_words, w1_scales, w3_words, w3_scales, gate, offs, pos1, pos2):
    idx = unstriped(offs)
    w2 = np.stack([unpack_weight(w2_words[e], w2_scales[e], "e2m1") for e in range(E)])
    w1 = np.stack([unpack_weight(w1_words[e], w1_scales[e], "e2m1") for e in range(E)])
    w3 = np.stack([unpack_weight(w3_words[e], w3_scales[e], "e2m1") for e in range(E)])
    gq = mxq(f64(gate) * f64(dyT)[:, idx], 0, "e4m3")
    dh = by_expert(w2, gq)
    da1 = dh * f64(a3) * d_relu(f64(a1))
    da3 = dh * relu(f64(a1))
    dx = by_expert(w1, mxq(da1, 0, "e4m3")) + by_expert(w3, mxq(da3, 0, "e4m3"))
    return dx[:, unstriped(pos1)] + dx[:, unstriped(pos2)]

@@ -1,0 +1,241 @@
+from contextlib import ExitStack
+
+import concourse.mybir as mybir
+from concourse.masks import make_identity
+
+K, T, E, C, H, N = 512, 512, 4, 256, 512, 1536
+P = 128
+S = N // 512
+CUTS = (0, 288, 768, 1024)
+SLOTS = E * C
+
+FLOPS = 2 * SLOTS * (N * H + 2 * H * K)
+BYTES = 11210752
+
+F32 = mybir.dt.float32
+BF16 = mybir.dt.bfloat16
+I32 = mybir.dt.int32
+U32 = mybir.dt.uint32
+U16 = mybir.dt.uint16
+U8 = mybir.dt.uint8
+FP8 = mybir.dt.float8_e4m3fn_x4
+FP4 = mybir.dt.float4_e2m1fn_x4
+MULT = mybir.AluOpType.mult
+ADD = mybir.AluOpType.add
+IS_GT = mybir.AluOpType.is_gt
+RELU = mybir.ActivationFunctionType.Relu
+SIGN = mybir.ActivationFunctionType.Sign
+
+
+def tile_moe_bdx_glu_relu_kernel(
+    tc, dyT, a1, a3, w2_words, w2_scales, w1_words, w1_scales, w3_words, w3_scales, gate, offs, pos1, pos2, out
+):
+    nc = tc.nc
+    with ExitStack() as ctx:
+        keep = ctx.enter_context(tc.tile_pool(name="keep", bufs=1))
+        work = ctx.enter_context(tc.tile_pool(name="work", bufs=3))
+        psum = ctx.enter_context(tc.psum_pool(name="psum", bufs=1))
+
+        offs_t = keep.tile([P, SLOTS // 16], U16, name="offs_t")
+        nc.sync.dma_start(offs_t[:], offs)
+
+        w2_pl = keep.tile([P, E * S, H], U8, name="w2_pl", align_bytes=64)
+        w1_pl = keep.tile([P, E, K], U8, name="w1_pl", align_bytes=64)
+        w3_pl = keep.tile([P, E, K], U8, name="w3_pl", align_bytes=64)
+        for pl in (w2_pl, w1_pl, w3_pl):
+            nc.vector.memset(pl[:].rearrange("p a b -> p (a b)").bitcast(I32), 0)
+        ident = keep.tile([P, P], F32, name="ident")
+        make_identity(nc, ident[:])
+
+        gates = []
+        planes = []
+        dy_v = dyT.rearrange("(s p t) c -> s t p c", p=P, t=4)
+        for c in range(3):
+            g = keep.tile([P, CUTS[c + 1] - CUTS[c]], F32, name=f"gate{c}")
+            gates.append(g)
+        for i in range(S * 4):
+            pt = keep.tile([P, T], F32, name=f"plane{i}")
+            planes.append(pt)
+        nc.scalar.dma_start(gates[0][:], gate[0:P, 0 : CUTS[1]])
+        nc.sync.dma_start(planes[0][:], dy_v[0, 0])
+        for i in range(1, S * 4):
+            nc.sync.dma_start(planes[i][:], dy_v[i // 4, i % 4])
+        w2_t = []
+        for e in range(E):
+            w = keep.tile([P, S, 2 * H], U8, name=f"w2_{e}", align_bytes=64)
+            w2_t.append(w)
+        w1_t = keep.tile([P, E, 2 * K], U8, name="w1_t", align_bytes=64)
+        w3_t = keep.tile([P, E, 2 * K], U8, name="w3_t", align_bytes=64)
+
+        def load_w2(e):
+            nc.sync.dma_start(w2_t[e][:].bitcast(I32), w2_words[e].bitcast(I32).rearrange("s p c -> p s c"))
+
+        a1_t, a3_t = [], []
+        for i in range(2):
+            x1 = keep.tile([P, 4, 2 * C], F32, name=f"a1_{i}")
+            x3 = keep.tile([P, 4, 2 * C], F32, name=f"a3_{i}")
+            a1_t.append(x1)
+            a3_t.append(x3)
+
+        def load_a(i):
+            nc.sync.dma_start(a1_t[i][:], a1.rearrange("(b p) j -> p b j", p=P)[:, :, 2 * C * i : 2 * C * (i + 1)])
+            nc.sync.dma_start(a3_t[i][:], a3.rearrange("(b p) j -> p b j", p=P)[:, :, 2 * C * i : 2 * C * (i + 1)])
+
+        load_w2(0)
+        for q in range(4):
+            nc.sync.dma_start(
+                w2_pl[32 * q : 32 * q + 4].bitcast(I32),
+                w2_scales.bitcast(I32).rearrange("e s f i -> f (e s) i")[4 * q : 4 * q + 4],
+            )
+        nc.sync.dma_start(gates[1][:], gate[0:P, CUTS[1] : CUTS[2]])
+        load_a(0)
+        for wt, ww in ((w1_t, w1_words), (w3_t, w3_words)):
+            nc.sync.dma_start(wt[:].bitcast(I32), ww.bitcast(I32).rearrange("e s p c -> p (e s) c"))
+        for pl, sc in ((w1_pl, w1_scales), (w3_pl, w3_scales)):
+            for q in range(4):
+                nc.sync.dma_start(
+                    pl[32 * q : 32 * q + 4].bitcast(I32),
+                    sc.bitcast(I32).rearrange("e s f i -> f (e s) i")[4 * q : 4 * q + 4],
+                )
+        load_w2(1)
+        load_w2(2)
+        nc.sync.dma_start(gates[2][:], gate[0:P, CUTS[2] : CUTS[3]])
+        load_a(1)
+        load_w2(3)
+        pos_t = []
+        for i, ps in enumerate((pos1, pos2)):
+            pp = keep.tile([P, T // 16], U16, name=f"pos_t{i}")
+            nc.sync.dma_start(pp[:], ps)
+            pos_t.append(pp)
+
+        dx = keep.tile([P, 4, SLOTS], F32, name="dx")
+
+        gf = []
+        for s in range(S):
+            g = keep.tile([P, 4, SLOTS], F32, name=f"gf{s}")
+            gf.append(g)
+        rm, gq, gs = {}, {}, {}
+
+        def saved(e):
+            for h in range(2):
+                col = C * (e % 2) + P * h
+                a1p = psum.tile([P, H], F32, name="a1p", bufs=1)
+                a3p = psum.tile([P, H], F32, name="a3p", bufs=1)
+                for b in range(4):
+                    nc.tensor.transpose(a1p[:, P * b : P * (b + 1)], a1_t[e // 2][:, b, col : col + P], ident[:])
+                for b in range(4):
+                    nc.tensor.transpose(a3p[:, P * b : P * (b + 1)], a3_t[e // 2][:, b, col : col + P], ident[:])
+                x = work.tile([P, 2, H], F32, name="rm", bufs=7)
+                nc.scalar.activation(x[:, 1, :], a1p[:], RELU)
+                nc.vector.scalar_tensor_tensor(x[:, 0, :], x[:, 1, :], 0.0, a3p[:], IS_GT, MULT)
+                rm[e, h] = x
+
+        def gather(c, s):
+            lo, hi = CUTS[c], CUTS[c + 1]
+            for t in range(4):
+                nc.vector.tensor_tensor(
+                    gf[s][:, t, lo:hi],
+                    planes[4 * s + t][:].indirect(offs_t[:, lo // 16 : hi // 16]),
+                    gates[c][:],
+                    MULT,
+                )
+
+        def quantize(e, s):
+            gb = work.tile([P, C, 4], BF16, name="gb", bufs=4, align_bytes=64)
+            nc.scalar.copy(
+                gb[:].rearrange("p (c i) t -> p c t i", i=4),
+                gf[s][:, :, C * e : C * (e + 1)].rearrange("p t (c i) -> p c t i", i=4),
+            )
+            q = work.tile([P, C], U32, name="gq", bufs=12, align_bytes=64)
+            z = work.tile([P, C], U8, name="gs", bufs=12, align_bytes=64)
+            nc.vector.quantize_mx(out=q[:].bitcast(FP8), scales=z[:], in_=gb[:].rearrange("p c t -> p (c t)"))
+            gq[e, s], gs[e, s] = q, z
+
+        def products(e, h):
+            sl = slice(P * h, P * (h + 1))
+            dh = psum.tile([P, H], F32, name="dh", bufs=2)
+            for s in range(S):
+                nc.tensor.matmul_mx(
+                    out=dh[:],
+                    lhsT=gq[e, s][:, sl].bitcast(FP8),
+                    lhsT_scale=gs[e, s][:, sl],
+                    rhs=w2_t[e][:, s, :].bitcast(FP4),
+                    rhs_scale=w2_pl[:, S * e + s, :],
+                    start=(s == 0),
+                    stop=(s == S - 1),
+                )
+            last = (e, h) == (E - 1, 1)
+            da = work.tile([P, 2, H], BF16, name="da", bufs=2, align_bytes=64)
+            if last:
+                for w in range(2):
+                    nc.vector.tensor_tensor(da[:, w, :], dh[:], rm[e, h][:, w, :], MULT)
+            else:
+                nc.vector.tensor_tensor(da[:], dh[:].unsqueeze(1).to_broadcast([P, 2, H]), rm[e, h][:], MULT)
+            words = (da[:, 0, :].bitcast(F32), da[:, 1, :].bitcast(F32))
+            dap = psum.tile([P, 2, 2, P], F32, name="dap", bufs=2)
+            for w in (0, 1):
+                for u in range(2):
+                    nc.tensor.transpose(dap[:, w, u, :], words[w][:, u:256:2], ident[:])
+            dag = work.tile([P, 2 * P * 4], BF16, name="dag", bufs=2, align_bytes=64)
+            dag_v = dag[:].bitcast(F32).rearrange("p (w r u) -> p w r u", w=2, u=2)
+            dap_v = dap[:].rearrange("p w u r -> p w r u")
+            dq = work.tile([P, 2 * P], U32, name="dq", bufs=2, align_bytes=64)
+            ds = work.tile([P, 2 * P], U8, name="ds", bufs=2, align_bytes=64)
+            if last:
+                for w in (1, 0):
+                    nc.scalar.copy(dag_v[:, w], dap_v[:, w])
+                    c = slice(P * w, P * (w + 1))
+                    nc.vector.quantize_mx(
+                        out=dq[:, c].bitcast(FP8), scales=ds[:, c], in_=dag[:, 512 * w : 512 * (w + 1)]
+                    )
+            else:
+                nc.scalar.copy(dag_v, dap_v)
+                nc.vector.quantize_mx(out=dq[:].bitcast(FP8), scales=ds[:], in_=dag[:])
+            dxp = psum.tile([P, 4, P], F32, name="dxp", bufs=2)
+            j0 = C * e + P * h
+            for kt in range(4):
+                for w, wt, pl in ((1, w3_t, w3_pl), (0, w1_t, w1_pl)):
+                    nc.tensor.matmul_mx(
+                        out=dxp[:, kt, :],
+                        lhsT=wt[:, e, 256 * kt : 256 * (kt + 1)].bitcast(FP4),
+                        lhsT_scale=pl[:, e, P * kt : P * (kt + 1)],
+                        rhs=dq[:, P * w : P * (w + 1)].bitcast(FP8),
+                        rhs_scale=ds[:, P * w : P * (w + 1)],
+                        start=(w == 1),
+                        stop=(w == 0),
+                    )
+                if last:
+                    nc.scalar.copy(dx[:, kt, j0 : j0 + P], dxp[:, kt, :])
+            if not last:
+                nc.scalar.copy(dx[:, :, j0 : j0 + P], dxp[:])
+
+        def chunk(c):
+            done = [e for e in range(E) if CUTS[c] < C * (e + 1) <= CUTS[c + 1]]
+            for s in range(S):
+                gather(c, s)
+                for e in done:
+                    quantize(e, s)
+
+        chunk(0)
+        saved(0)
+        for h in range(2):
+            products(0, h)
+        chunk(1)
+        saved(1)
+        saved(2)
+        for h in range(2):
+            products(1, h)
+        saved(3)
+        chunk(2)
+        for e in (2, 3):
+            for h in range(2):
+                products(e, h)
+
+        for kt in range(4):
+            o1 = work.tile([P, T], F32, name="o1", bufs=2)
+            o2 = work.tile([P, T], F32, name="o2", bufs=2)
+            o = work.tile([P, T], F32, name="o", bufs=2)
+            nc.vector.tensor_copy(o1[:], dx[:, kt, :].indirect(pos_t[0][:]))
+            nc.vector.tensor_copy(o2[:], dx[:, kt, :].indirect(pos_t[1][:]))
+            (nc.vector if kt == 3 else nc.gpsimd).tensor_tensor(o[:], o1[:], o2[:], ADD)
+            nc.sync.dma_start(out[P * kt : P * (kt + 1), :], o[:])

@@ -6,7 +6,6 @@ from concourse.masks import make_identity
 K, T, E, C, H, N = 512, 512, 4, 256, 512, 1536
 P = 128
 S = N // 512
-CUTS = (0, 288, 768, 1024)
 SLOTS = E * C
 
 FLOPS = 2 * SLOTS * (N * H + 2 * H * K)
@@ -24,7 +23,29 @@ MULT = mybir.AluOpType.mult
 ADD = mybir.AluOpType.add
 IS_GT = mybir.AluOpType.is_gt
 RELU = mybir.ActivationFunctionType.Relu
-SIGN = mybir.ActivationFunctionType.Sign
+
+PROGRAM = (
+    ("g", 0, 0, 0, -1), ("g", 0, 0, 1, -1), ("g", 0, 0, 2, -1), ("g", 0, 0, 3, -1), ("g", 0, 1, 0, -1),
+    ("g", 0, 1, 1, -1), ("g", 0, 1, 2, -1), ("g", 0, 1, 3, -1), ("g", 0, 2, 0, -1), ("g", 0, 2, 1, -1),
+    ("g", 0, 2, 2, -1), ("g", 0, 2, 3, -1), ("g", 1, 0, 0, -1), ("g", 1, 0, 1, -1), ("q", 0, 256, 1),
+    ("q", 0, 256, 0), ("g", 1, 0, 2, -1), ("g", 1, 0, 3, -1), ("q", 0, 256, 2), ("g", 1, 1, 0, -1),
+    ("g", 1, 1, 1, -1), ("g", 1, 1, 2, -1), ("g", 1, 1, 3, -1), ("g", 1, 2, 0, -1), ("g", 1, 2, 1, -1),
+    ("m", 0), ("g", 1, 2, 2, -1), ("g", 1, 2, 3, -1), ("q", 256, 512, 0), ("dh", 0),
+    ("da", 0), ("g", 2, 0, 0, -1), ("dh", 1), ("q", 256, 512, 1), ("g", 2, 0, 1, -1),
+    ("g", 2, 0, 2, -1), ("g", 2, 0, 3, -1), ("g", 2, 1, 0, -1), ("m", 1), ("da", 1),
+    ("g", 2, 1, 1, -1), ("g", 2, 1, 2, -1), ("g", 2, 1, 3, -1), ("g", 2, 2, 0, -1), ("g", 2, 2, 1, -1),
+    ("g", 2, 2, 2, -1), ("q", 256, 512, 2), ("g", 2, 2, 3, -1), ("g", 3, 0, 0, -1), ("m", 2),
+    ("q", 512, 768, 0), ("g", 3, 0, 1, -1), ("g", 3, 0, 2, -1), ("g", 3, 0, 3, -1), ("dh", 2),
+    ("dq", 0), ("g", 3, 1, 0, -1), ("dq", 1), ("da", 2), ("dh", 3),
+    ("m", 3), ("da", 3), ("g", 3, 1, 1, -1), ("g", 3, 1, 2, -1), ("q", 512, 768, 1),
+    ("g", 3, 1, 3, -1), ("q", 512, 768, 2), ("g", 3, 2, 0, 0), ("dh", 4), ("q", 768, 1024, 0),
+    ("g", 3, 2, 1, 0), ("g", 3, 2, 2, 0), ("m", 4), ("dq", 2), ("dh", 5),
+    ("da", 4), ("dq", 3), ("g", 3, 2, 3, 0), ("m", 5), ("g", 3, 2, 0, 1),
+    ("q", 768, 1024, 1), ("da", 5), ("q", 768, 896, 2), ("m", 6), ("g", 3, 2, 1, 1),
+    ("dh", 6), ("g", 3, 2, 2, 1), ("dq", 4), ("g", 3, 2, 3, 1), ("q", 896, 1024, 2),
+    ("dh", 7), ("da", 6), ("dq", 5), ("m", 7), ("da", 7),
+    ("dq", 6), ("dq", 7),
+)
 
 
 def tile_moe_bdx_glu_relu_kernel(
@@ -47,61 +68,56 @@ def tile_moe_bdx_glu_relu_kernel(
         ident = keep.tile([P, P], F32, name="ident")
         make_identity(nc, ident[:])
 
-        gates = []
-        planes = []
+        gates, planes, w2_t, a1_t, a3_t = [], [], [], [], []
         dy_v = dyT.rearrange("(s p t) c -> s t p c", p=P, t=4)
-        for c in range(3):
-            g = keep.tile([P, CUTS[c + 1] - CUTS[c]], F32, name=f"gate{c}")
-            gates.append(g)
+        g0 = keep.tile([P, C], F32, name="gate_a")
+        g1 = keep.tile([P, 3 * C], F32, name="gate_b")
+        gates = [g0[:]] + [g1[:, C * i : C * (i + 1)] for i in range(3)]
         for i in range(S * 4):
             pt = keep.tile([P, T], F32, name=f"plane{i}")
             planes.append(pt)
-        nc.scalar.dma_start(gates[0][:], gate[0:P, 0 : CUTS[1]])
-        nc.sync.dma_start(planes[0][:], dy_v[0, 0])
-        for i in range(1, S * 4):
-            nc.sync.dma_start(planes[i][:], dy_v[i // 4, i % 4])
-        w2_t = []
         for e in range(E):
             w = keep.tile([P, S, 2 * H], U8, name=f"w2_{e}", align_bytes=64)
             w2_t.append(w)
         w1_t = keep.tile([P, E, 2 * K], U8, name="w1_t", align_bytes=64)
         w3_t = keep.tile([P, E, 2 * K], U8, name="w3_t", align_bytes=64)
+        for e in range(E):
+            x1 = keep.tile([P, 4, C], F32, name=f"a1_{e}")
+            x3 = keep.tile([P, 4, C], F32, name=f"a3_{e}")
+            a1_t.append(x1)
+            a3_t.append(x3)
 
         def load_w2(e):
             nc.sync.dma_start(w2_t[e][:].bitcast(I32), w2_words[e].bitcast(I32).rearrange("s p c -> p s c"))
 
-        a1_t, a3_t = [], []
-        for i in range(2):
-            x1 = keep.tile([P, 4, 2 * C], F32, name=f"a1_{i}")
-            x3 = keep.tile([P, 4, 2 * C], F32, name=f"a3_{i}")
-            a1_t.append(x1)
-            a3_t.append(x3)
+        def load_a(e):
+            nc.sync.dma_start(a1_t[e][:], a1.rearrange("(b p) j -> p b j", p=P)[:, :, C * e : C * (e + 1)])
+            nc.sync.dma_start(a3_t[e][:], a3.rearrange("(b p) j -> p b j", p=P)[:, :, C * e : C * (e + 1)])
 
-        def load_a(i):
-            nc.sync.dma_start(a1_t[i][:], a1.rearrange("(b p) j -> p b j", p=P)[:, :, 2 * C * i : 2 * C * (i + 1)])
-            nc.sync.dma_start(a3_t[i][:], a3.rearrange("(b p) j -> p b j", p=P)[:, :, 2 * C * i : 2 * C * (i + 1)])
-
-        load_w2(0)
-        for q in range(4):
-            nc.sync.dma_start(
-                w2_pl[32 * q : 32 * q + 4].bitcast(I32),
-                w2_scales.bitcast(I32).rearrange("e s f i -> f (e s) i")[4 * q : 4 * q + 4],
-            )
-        nc.sync.dma_start(gates[1][:], gate[0:P, CUTS[1] : CUTS[2]])
-        load_a(0)
-        for wt, ww in ((w1_t, w1_words), (w3_t, w3_words)):
-            nc.sync.dma_start(wt[:].bitcast(I32), ww.bitcast(I32).rearrange("e s p c -> p (e s) c"))
-        for pl, sc in ((w1_pl, w1_scales), (w3_pl, w3_scales)):
+        def load_scales(pl, sc):
             for q in range(4):
                 nc.sync.dma_start(
                     pl[32 * q : 32 * q + 4].bitcast(I32),
                     sc.bitcast(I32).rearrange("e s f i -> f (e s) i")[4 * q : 4 * q + 4],
                 )
+
+        nc.scalar.dma_start(g0[:], gate[0:P, 0:C])
+        for i in range(S * 4):
+            nc.sync.dma_start(planes[i][:], dy_v[i // 4, i % 4])
+        nc.sync.dma_start(g1[:], gate[0:P, C:SLOTS])
+        load_w2(0)
+        load_scales(w2_pl, w2_scales)
+        load_a(0)
+        for wt, ww in ((w1_t, w1_words), (w3_t, w3_words)):
+            nc.sync.dma_start(wt[:].bitcast(I32), ww.bitcast(I32).rearrange("e s p c -> p (e s) c"))
+        load_scales(w1_pl, w1_scales)
+        load_scales(w3_pl, w3_scales)
         load_w2(1)
-        load_w2(2)
-        nc.sync.dma_start(gates[2][:], gate[0:P, CUTS[2] : CUTS[3]])
         load_a(1)
+        load_w2(2)
+        load_a(2)
         load_w2(3)
+        load_a(3)
         pos_t = []
         for i, ps in enumerate((pos1, pos2)):
             pp = keep.tile([P, T // 16], U16, name=f"pos_t{i}")
@@ -109,127 +125,119 @@ def tile_moe_bdx_glu_relu_kernel(
             pos_t.append(pp)
 
         dx = keep.tile([P, 4, SLOTS], F32, name="dx")
-
-        gf = []
+        gq, gs = [], []
         for s in range(S):
-            g = keep.tile([P, 4, SLOTS], F32, name=f"gf{s}")
-            gf.append(g)
-        rm, gq, gs = {}, {}, {}
+            q = keep.tile([P, SLOTS], U32, name=f"gq{s}", align_bytes=64)
+            z = keep.tile([P, SLOTS], U8, name=f"gs{s}", align_bytes=64)
+            gq.append(q)
+            gs.append(z)
+        gf, gb, rm, dh, dag, dq, ds = {}, {}, {}, {}, {}, {}, {}
 
-        def saved(e):
-            for h in range(2):
-                col = C * (e % 2) + P * h
-                a1p = psum.tile([P, H], F32, name="a1p", bufs=1)
-                a3p = psum.tile([P, H], F32, name="a3p", bufs=1)
-                for b in range(4):
-                    nc.tensor.transpose(a1p[:, P * b : P * (b + 1)], a1_t[e // 2][:, b, col : col + P], ident[:])
-                for b in range(4):
-                    nc.tensor.transpose(a3p[:, P * b : P * (b + 1)], a3_t[e // 2][:, b, col : col + P], ident[:])
-                x = work.tile([P, 2, H], F32, name="rm", bufs=7)
-                nc.scalar.activation(x[:, 1, :], a1p[:], RELU)
-                nc.vector.scalar_tensor_tensor(x[:, 0, :], x[:, 1, :], 0.0, a3p[:], IS_GT, MULT)
-                rm[e, h] = x
-
-        def gather(c, s):
-            lo, hi = CUTS[c], CUTS[c + 1]
-            for t in range(4):
-                nc.vector.tensor_tensor(
-                    gf[s][:, t, lo:hi],
-                    planes[4 * s + t][:].indirect(offs_t[:, lo // 16 : hi // 16]),
-                    gates[c][:],
-                    MULT,
-                )
-
-        def quantize(e, s):
-            gb = work.tile([P, C, 4], BF16, name="gb", bufs=4, align_bytes=64)
-            nc.scalar.copy(
-                gb[:].rearrange("p (c i) t -> p c t i", i=4),
-                gf[s][:, :, C * e : C * (e + 1)].rearrange("p t (c i) -> p c t i", i=4),
+        def gather(e, s, t, half):
+            lo, hi = (0, C) if half < 0 else (P * half, P * (half + 1))
+            if t == 0 and half <= 0:
+                g = work.tile([P, 4, C], F32, name="gf", bufs=5)
+                gf[e, s] = g
+            nc.vector.tensor_tensor(
+                gf[e, s][:, t, lo:hi],
+                planes[4 * s + t][:].indirect(offs_t[:, (C * e + lo) // 16 : (C * e + hi) // 16]),
+                gates[e][:, lo:hi],
+                MULT,
             )
-            q = work.tile([P, C], U32, name="gq", bufs=12, align_bytes=64)
-            z = work.tile([P, C], U8, name="gs", bufs=12, align_bytes=64)
-            nc.vector.quantize_mx(out=q[:].bitcast(FP8), scales=z[:], in_=gb[:].rearrange("p c t -> p (c t)"))
-            gq[e, s], gs[e, s] = q, z
+            if t == 3:
+                b = work.tile([P, C, 4], BF16, name="gb", bufs=5, align_bytes=64)
+                nc.scalar.copy(
+                    b[:, 0 : hi - lo, :].rearrange("p (c i) t -> p c t i", i=4),
+                    gf[e, s][:, :, lo:hi].rearrange("p t (c i) -> p c t i", i=4),
+                )
+                gb[C * e + lo, s] = b
 
-        def products(e, h):
-            sl = slice(P * h, P * (h + 1))
-            dh = psum.tile([P, H], F32, name="dh", bufs=2)
+        def quantize(lo, hi, s):
+            nc.vector.quantize_mx(
+                out=gq[s][:, lo:hi].bitcast(FP8),
+                scales=gs[s][:, lo:hi],
+                in_=gb[lo, s][:, 0 : hi - lo, :].rearrange("p c t -> p (c t)"),
+            )
+
+        def saved(i):
+            e, col = i // 2, P * (i % 2)
+            a1p = psum.tile([P, H], F32, name="a1p", bufs=1)
+            a3p = psum.tile([P, H], F32, name="a3p", bufs=1)
+            for b in range(4):
+                nc.tensor.transpose(a1p[:, P * b : P * (b + 1)], a1_t[e][:, b, col : col + P], ident[:])
+            for b in range(4):
+                nc.tensor.transpose(a3p[:, P * b : P * (b + 1)], a3_t[e][:, b, col : col + P], ident[:])
+            x = work.tile([P, 2, H], F32, name="rm", bufs=6)
+            nc.scalar.activation(x[:, 1, :], a1p[:], RELU)
+            nc.vector.scalar_tensor_tensor(x[:, 0, :], x[:, 1, :], 0.0, a3p[:], IS_GT, MULT)
+            rm[i] = x
+
+        def first(i):
+            sl = slice(P * i, P * (i + 1))
+            e = i // 2
+            acc = psum.tile([P, H], F32, name="dh", bufs=2)
             for s in range(S):
                 nc.tensor.matmul_mx(
-                    out=dh[:],
-                    lhsT=gq[e, s][:, sl].bitcast(FP8),
-                    lhsT_scale=gs[e, s][:, sl],
+                    out=acc[:],
+                    lhsT=gq[s][:, sl].bitcast(FP8),
+                    lhsT_scale=gs[s][:, sl],
                     rhs=w2_t[e][:, s, :].bitcast(FP4),
                     rhs_scale=w2_pl[:, S * e + s, :],
                     start=(s == 0),
                     stop=(s == S - 1),
                 )
-            last = (e, h) == (E - 1, 1)
-            da = work.tile([P, 2, H], BF16, name="da", bufs=2, align_bytes=64)
+            dh[i] = acc
+
+        def grads(i):
+            last = i == 7
+            da = work.tile([P, 2, H], BF16, name="da", bufs=3, align_bytes=64)
             if last:
                 for w in range(2):
-                    nc.vector.tensor_tensor(da[:, w, :], dh[:], rm[e, h][:, w, :], MULT)
+                    nc.vector.tensor_tensor(da[:, w, :], dh[i][:], rm[i][:, w, :], MULT)
             else:
-                nc.vector.tensor_tensor(da[:], dh[:].unsqueeze(1).to_broadcast([P, 2, H]), rm[e, h][:], MULT)
-            words = (da[:, 0, :].bitcast(F32), da[:, 1, :].bitcast(F32))
+                nc.vector.tensor_tensor(da[:], dh[i][:].unsqueeze(1).to_broadcast([P, 2, H]), rm[i][:], MULT)
             dap = psum.tile([P, 2, 2, P], F32, name="dap", bufs=2)
-            for w in (0, 1):
+            for w in range(2):
+                words = da[:, w, :].bitcast(F32)
                 for u in range(2):
-                    nc.tensor.transpose(dap[:, w, u, :], words[w][:, u:256:2], ident[:])
-            dag = work.tile([P, 2 * P * 4], BF16, name="dag", bufs=2, align_bytes=64)
-            dag_v = dag[:].bitcast(F32).rearrange("p (w r u) -> p w r u", w=2, u=2)
+                    nc.tensor.transpose(dap[:, w, u, :], words[:, u:256:2], ident[:])
+            g = work.tile([P, 2 * P * 4], BF16, name="dag", bufs=3, align_bytes=64)
+            g_v = g[:].bitcast(F32).rearrange("p (w r u) -> p w r u", w=2, u=2)
             dap_v = dap[:].rearrange("p w u r -> p w r u")
-            dq = work.tile([P, 2 * P], U32, name="dq", bufs=2, align_bytes=64)
-            ds = work.tile([P, 2 * P], U8, name="ds", bufs=2, align_bytes=64)
             if last:
-                for w in (1, 0):
-                    nc.scalar.copy(dag_v[:, w], dap_v[:, w])
-                    c = slice(P * w, P * (w + 1))
-                    nc.vector.quantize_mx(
-                        out=dq[:, c].bitcast(FP8), scales=ds[:, c], in_=dag[:, 512 * w : 512 * (w + 1)]
-                    )
+                for w in range(2):
+                    nc.scalar.copy(g_v[:, w], dap_v[:, w])
             else:
-                nc.scalar.copy(dag_v, dap_v)
-                nc.vector.quantize_mx(out=dq[:].bitcast(FP8), scales=ds[:], in_=dag[:])
+                nc.scalar.copy(g_v, dap_v)
+            dag[i] = g
+
+        def second(i):
+            last = i == 7
+            q = work.tile([P, 2 * P], U32, name="dq", bufs=3, align_bytes=64)
+            z = work.tile([P, 2 * P], U8, name="ds", bufs=3, align_bytes=64)
+            for a, b in ((0, P), (P, 2 * P)) if last else ((0, 2 * P),):
+                nc.vector.quantize_mx(out=q[:, a:b].bitcast(FP8), scales=z[:, a:b], in_=dag[i][:, 4 * a : 4 * b])
             dxp = psum.tile([P, 4, P], F32, name="dxp", bufs=2)
-            j0 = C * e + P * h
+            j0 = P * i
             for kt in range(4):
-                for w, wt, pl in ((1, w3_t, w3_pl), (0, w1_t, w1_pl)):
+                for w, (wt, pl) in enumerate(((w1_t, w1_pl), (w3_t, w3_pl))):
                     nc.tensor.matmul_mx(
                         out=dxp[:, kt, :],
-                        lhsT=wt[:, e, 256 * kt : 256 * (kt + 1)].bitcast(FP4),
-                        lhsT_scale=pl[:, e, P * kt : P * (kt + 1)],
-                        rhs=dq[:, P * w : P * (w + 1)].bitcast(FP8),
-                        rhs_scale=ds[:, P * w : P * (w + 1)],
-                        start=(w == 1),
-                        stop=(w == 0),
+                        lhsT=wt[:, i // 2, 256 * kt : 256 * (kt + 1)].bitcast(FP4),
+                        lhsT_scale=pl[:, i // 2, P * kt : P * (kt + 1)],
+                        rhs=q[:, P * w : P * (w + 1)].bitcast(FP8),
+                        rhs_scale=z[:, P * w : P * (w + 1)],
+                        start=(w == 0),
+                        stop=(w == 1),
                     )
                 if last:
                     nc.scalar.copy(dx[:, kt, j0 : j0 + P], dxp[:, kt, :])
             if not last:
                 nc.scalar.copy(dx[:, :, j0 : j0 + P], dxp[:])
 
-        def chunk(c):
-            done = [e for e in range(E) if CUTS[c] < C * (e + 1) <= CUTS[c + 1]]
-            for s in range(S):
-                gather(c, s)
-                for e in done:
-                    quantize(e, s)
-
-        chunk(0)
-        saved(0)
-        for h in range(2):
-            products(0, h)
-        chunk(1)
-        saved(1)
-        saved(2)
-        for h in range(2):
-            products(1, h)
-        saved(3)
-        chunk(2)
-        for e in (2, 3):
-            for h in range(2):
-                products(e, h)
+        steps = {"g": gather, "q": quantize, "m": saved, "dh": first, "da": grads, "dq": second}
+        for step in PROGRAM:
+            steps[step[0]](*step[1:])
 
         for kt in range(4):
             o1 = work.tile([P, T], F32, name="o1", bufs=2)

@@ -81,9 +81,9 @@ def tile_moe_bdx_glu_relu_kernel(
             w2_t.append(w)
         w1_t = keep.tile([P, E, 2 * K], U8, name="w1_t", align_bytes=64)
         w3_t = keep.tile([P, E, 2 * K], U8, name="w3_t", align_bytes=64)
-        for e in range(E):
-            x1 = keep.tile([P, 4, C], F32, name=f"a1_{e}")
-            x3 = keep.tile([P, 4, C], F32, name=f"a3_{e}")
+        for e in range(2):
+            x1 = keep.tile([P, 4, 2 * C], F32, name=f"a1_{e}")
+            x3 = keep.tile([P, 4, 2 * C], F32, name=f"a3_{e}")
             a1_t.append(x1)
             a3_t.append(x3)
 
@@ -91,8 +91,9 @@ def tile_moe_bdx_glu_relu_kernel(
             nc.sync.dma_start(w2_t[e][:].bitcast(I32), w2_words[e].bitcast(I32).rearrange("s p c -> p s c"))
 
         def load_a(e):
-            nc.sync.dma_start(a1_t[e][:], a1.rearrange("(b p) j -> p b j", p=P)[:, :, C * e : C * (e + 1)])
-            nc.sync.dma_start(a3_t[e][:], a3.rearrange("(b p) j -> p b j", p=P)[:, :, C * e : C * (e + 1)])
+            queue = nc.scalar if e == 0 else nc.sync
+            queue.dma_start(a1_t[e][:], a1.rearrange("(b p) j -> p b j", p=P)[:, :, 2 * C * e : 2 * C * (e + 1)])
+            queue.dma_start(a3_t[e][:], a3.rearrange("(b p) j -> p b j", p=P)[:, :, 2 * C * e : 2 * C * (e + 1)])
 
         def load_scales(pl, sc):
             for q in range(4):
@@ -103,21 +104,19 @@ def tile_moe_bdx_glu_relu_kernel(
 
         nc.scalar.dma_start(g0[:], gate[0:P, 0:C])
         for i in range(S * 4):
-            nc.sync.dma_start(planes[i][:], dy_v[i // 4, i % 4])
-        nc.sync.dma_start(g1[:], gate[0:P, C:SLOTS])
+            (nc.scalar if i % 2 else nc.sync).dma_start(planes[i][:], dy_v[i // 4, i % 4])
+        nc.scalar.dma_start(g1[:], gate[0:P, C:SLOTS])
+        load_a(0)
         load_w2(0)
         load_scales(w2_pl, w2_scales)
-        load_a(0)
         for wt, ww in ((w1_t, w1_words), (w3_t, w3_words)):
             nc.sync.dma_start(wt[:].bitcast(I32), ww.bitcast(I32).rearrange("e s p c -> p (e s) c"))
         load_scales(w1_pl, w1_scales)
         load_scales(w3_pl, w3_scales)
         load_w2(1)
-        load_a(1)
         load_w2(2)
-        load_a(2)
+        load_a(1)
         load_w2(3)
-        load_a(3)
         pos_t = []
         for i, ps in enumerate((pos1, pos2)):
             pp = keep.tile([P, T // 16], U16, name=f"pos_t{i}")
@@ -125,12 +124,7 @@ def tile_moe_bdx_glu_relu_kernel(
             pos_t.append(pp)
 
         dx = keep.tile([P, 4, SLOTS], F32, name="dx")
-        gq, gs = [], []
-        for s in range(S):
-            q = keep.tile([P, SLOTS], U32, name=f"gq{s}", align_bytes=64)
-            z = keep.tile([P, SLOTS], U8, name=f"gs{s}", align_bytes=64)
-            gq.append(q)
-            gs.append(z)
+        gq, gs = {}, {}
         gf, gb, rm, dh, dag, dq, ds = {}, {}, {}, {}, {}, {}, {}
 
         def gather(e, s, t, half):
@@ -153,14 +147,19 @@ def tile_moe_bdx_glu_relu_kernel(
                 gb[C * e + lo, s] = b
 
         def quantize(lo, hi, s):
+            q = keep.tile([P, hi - lo], U32, name=f"gq{s}_{lo}", align_bytes=64)
+            z = keep.tile([P, hi - lo], U8, name=f"gs{s}_{lo}", align_bytes=64)
+            for i in range(lo // P, hi // P):
+                gq[i, s] = q[:, P * i - lo : P * i - lo + P]
+                gs[i, s] = z[:, P * i - lo : P * i - lo + P]
             nc.vector.quantize_mx(
-                out=gq[s][:, lo:hi].bitcast(FP8),
-                scales=gs[s][:, lo:hi],
+                out=q[:].bitcast(FP8),
+                scales=z[:],
                 in_=gb[lo, s][:, 0 : hi - lo, :].rearrange("p c t -> p (c t)"),
             )
 
         def saved(i):
-            e, col = i // 2, P * (i % 2)
+            e, col = i // 4, P * (i % 4)
             a1p = psum.tile([P, H], F32, name="a1p", bufs=1)
             a3p = psum.tile([P, H], F32, name="a3p", bufs=1)
             for b in range(4):
@@ -173,14 +172,13 @@ def tile_moe_bdx_glu_relu_kernel(
             rm[i] = x
 
         def first(i):
-            sl = slice(P * i, P * (i + 1))
             e = i // 2
             acc = psum.tile([P, H], F32, name="dh", bufs=2)
             for s in range(S):
                 nc.tensor.matmul_mx(
                     out=acc[:],
-                    lhsT=gq[s][:, sl].bitcast(FP8),
-                    lhsT_scale=gs[s][:, sl],
+                    lhsT=gq[i, s].bitcast(FP8),
+                    lhsT_scale=gs[i, s],
                     rhs=w2_t[e][:, s, :].bitcast(FP4),
                     rhs_scale=w2_pl[:, S * e + s, :],
                     start=(s == 0),

@@ -7,6 +7,8 @@ K, T, E, C, H, N = 512, 512, 4, 256, 512, 1536
 P = 128
 S = N // 512
 SLOTS = E * C
+CUT = 384
+PIECES = ((0, 256), (256, 384), (384, 512), (512, 768), (768, 896), (768, 1024), (896, 1024))
 
 FLOPS = 2 * SLOTS * (N * H + 2 * H * K)
 BYTES = 11210752
@@ -25,26 +27,28 @@ IS_GT = mybir.AluOpType.is_gt
 RELU = mybir.ActivationFunctionType.Relu
 
 PROGRAM = (
-    ("g", 0, 0, 0, -1), ("g", 0, 0, 1, -1), ("g", 0, 0, 2, -1), ("g", 0, 0, 3, -1), ("g", 0, 1, 0, -1),
-    ("g", 0, 1, 1, -1), ("g", 0, 1, 2, -1), ("g", 0, 1, 3, -1), ("g", 0, 2, 0, -1), ("g", 0, 2, 1, -1),
-    ("g", 0, 2, 2, -1), ("g", 0, 2, 3, -1), ("g", 1, 0, 0, -1), ("g", 1, 0, 1, -1), ("q", 0, 256, 1),
-    ("q", 0, 256, 0), ("g", 1, 0, 2, -1), ("g", 1, 0, 3, -1), ("q", 0, 256, 2), ("g", 1, 1, 0, -1),
-    ("g", 1, 1, 1, -1), ("g", 1, 1, 2, -1), ("g", 1, 1, 3, -1), ("g", 1, 2, 0, -1), ("g", 1, 2, 1, -1),
-    ("m", 0), ("g", 1, 2, 2, -1), ("g", 1, 2, 3, -1), ("q", 256, 512, 0), ("dh", 0),
-    ("da", 0), ("g", 2, 0, 0, -1), ("dh", 1), ("q", 256, 512, 1), ("g", 2, 0, 1, -1),
-    ("g", 2, 0, 2, -1), ("g", 2, 0, 3, -1), ("g", 2, 1, 0, -1), ("m", 1), ("da", 1),
-    ("g", 2, 1, 1, -1), ("g", 2, 1, 2, -1), ("g", 2, 1, 3, -1), ("g", 2, 2, 0, -1), ("g", 2, 2, 1, -1),
-    ("g", 2, 2, 2, -1), ("q", 256, 512, 2), ("g", 2, 2, 3, -1), ("g", 3, 0, 0, -1), ("m", 2),
-    ("q", 512, 768, 0), ("g", 3, 0, 1, -1), ("g", 3, 0, 2, -1), ("g", 3, 0, 3, -1), ("dh", 2),
-    ("dq", 0), ("g", 3, 1, 0, -1), ("dq", 1), ("da", 2), ("dh", 3),
-    ("m", 3), ("da", 3), ("g", 3, 1, 1, -1), ("g", 3, 1, 2, -1), ("q", 512, 768, 1),
-    ("g", 3, 1, 3, -1), ("q", 512, 768, 2), ("g", 3, 2, 0, 0), ("dh", 4), ("q", 768, 1024, 0),
-    ("g", 3, 2, 1, 0), ("g", 3, 2, 2, 0), ("m", 4), ("dq", 2), ("dh", 5),
-    ("da", 4), ("dq", 3), ("g", 3, 2, 3, 0), ("m", 5), ("g", 3, 2, 0, 1),
-    ("q", 768, 1024, 1), ("da", 5), ("q", 768, 896, 2), ("m", 6), ("g", 3, 2, 1, 1),
-    ("dh", 6), ("g", 3, 2, 2, 1), ("dq", 4), ("g", 3, 2, 3, 1), ("q", 896, 1024, 2),
-    ("dh", 7), ("da", 6), ("dq", 5), ("m", 7), ("da", 7),
-    ("dq", 6), ("dq", 7),
+    ("g", 0, 0, 0, 0, 384), ("g", 0, 0, 1, 0, 384), ("g", 0, 0, 2, 0, 384), ("g", 0, 0, 3, 0, 384),
+    ("m", 0), ("g", 0, 1, 0, 0, 384), ("g", 0, 1, 1, 0, 384), ("g", 0, 1, 2, 0, 384),
+    ("g", 0, 1, 3, 0, 384), ("g", 0, 2, 0, 0, 384), ("g", 0, 2, 1, 0, 384), ("g", 0, 2, 2, 0, 384),
+    ("m", 1), ("g", 0, 2, 3, 0, 384), ("g", 1, 0, 0, 384, 768), ("q", 256, 384, 0),
+    ("q", 256, 384, 1), ("g", 1, 0, 1, 384, 768), ("q", 0, 256, 1), ("g", 1, 0, 2, 384, 768),
+    ("q", 0, 256, 2), ("q", 256, 384, 2), ("q", 0, 256, 0), ("g", 1, 0, 3, 384, 768),
+    ("g", 1, 1, 0, 384, 768), ("m", 2), ("q", 384, 512, 0), ("g", 1, 1, 1, 384, 768),
+    ("g", 1, 1, 2, 384, 768), ("g", 1, 1, 3, 384, 768), ("dh", 0), ("da", 0),
+    ("g", 1, 2, 0, 384, 768), ("g", 1, 2, 1, 384, 768), ("q", 384, 512, 1), ("g", 1, 2, 2, 384, 768),
+    ("g", 1, 2, 3, 384, 768), ("dh", 1), ("dh", 2), ("da", 1),
+    ("dq", 0), ("g", 2, 0, 0, 768, 1024), ("m", 3), ("q", 384, 512, 2),
+    ("q", 512, 768, 0), ("g", 2, 0, 1, 768, 1024), ("dh", 3), ("da", 2),
+    ("g", 2, 0, 2, 768, 1024), ("g", 2, 0, 3, 768, 1024), ("g", 2, 1, 0, 768, 1024), ("m", 4),
+    ("da", 3), ("g", 2, 1, 1, 768, 1024), ("g", 2, 1, 2, 768, 1024), ("q", 512, 768, 1),
+    ("m", 5), ("g", 2, 1, 3, 768, 1024), ("q", 512, 768, 2), ("g", 2, 2, 0, 768, 896),
+    ("g", 2, 2, 1, 768, 896), ("dq", 1), ("g", 2, 2, 2, 768, 896), ("dh", 4),
+    ("dq", 2), ("dh", 5), ("g", 2, 2, 3, 768, 896), ("m", 6),
+    ("da", 4), ("q", 768, 1024, 0), ("da", 5), ("q", 768, 1024, 1),
+    ("g", 2, 2, 0, 896, 1024), ("g", 2, 2, 1, 896, 1024), ("g", 2, 2, 2, 896, 1024), ("g", 2, 2, 3, 896, 1024),
+    ("q", 768, 896, 2), ("dq", 3), ("dh", 6), ("q", 896, 1024, 2),
+    ("m", 7), ("dh", 7), ("dq", 4), ("da", 6),
+    ("da", 7), ("dq", 5), ("dq", 6), ("dq", 7),
 )
 
 
@@ -70,9 +74,8 @@ def tile_moe_bdx_glu_relu_kernel(
 
         gates, planes, w2_t, a1_t, a3_t = [], [], [], [], []
         dy_v = dyT.rearrange("(s p t) c -> s t p c", p=P, t=4)
-        g0 = keep.tile([P, C], F32, name="gate_a")
-        g1 = keep.tile([P, 3 * C], F32, name="gate_b")
-        gates = [g0[:]] + [g1[:, C * i : C * (i + 1)] for i in range(3)]
+        g0 = keep.tile([P, CUT], F32, name="gate_a")
+        g1 = keep.tile([P, SLOTS - CUT], F32, name="gate_b")
         for i in range(S * 4):
             pt = keep.tile([P, T], F32, name=f"plane{i}")
             planes.append(pt)
@@ -91,9 +94,8 @@ def tile_moe_bdx_glu_relu_kernel(
             nc.sync.dma_start(w2_t[e][:].bitcast(I32), w2_words[e].bitcast(I32).rearrange("s p c -> p s c"))
 
         def load_a(e):
-            queue = nc.scalar if e == 0 else nc.sync
-            queue.dma_start(a1_t[e][:], a1.rearrange("(b p) j -> p b j", p=P)[:, :, 2 * C * e : 2 * C * (e + 1)])
-            queue.dma_start(a3_t[e][:], a3.rearrange("(b p) j -> p b j", p=P)[:, :, 2 * C * e : 2 * C * (e + 1)])
+            nc.scalar.dma_start(a1_t[e][:], a1.rearrange("(b p) j -> p b j", p=P)[:, :, 2 * C * e : 2 * C * (e + 1)])
+            nc.scalar.dma_start(a3_t[e][:], a3.rearrange("(b p) j -> p b j", p=P)[:, :, 2 * C * e : 2 * C * (e + 1)])
 
         def load_scales(pl, sc):
             for q in range(4):
@@ -102,20 +104,19 @@ def tile_moe_bdx_glu_relu_kernel(
                     sc.bitcast(I32).rearrange("e s f i -> f (e s) i")[4 * q : 4 * q + 4],
                 )
 
-        nc.scalar.dma_start(g0[:], gate[0:P, 0:C])
+        nc.scalar.dma_start(g0[:], gate[0:P, 0:CUT])
         for i in range(S * 4):
             (nc.scalar if i % 2 else nc.sync).dma_start(planes[i][:], dy_v[i // 4, i % 4])
-        nc.scalar.dma_start(g1[:], gate[0:P, C:SLOTS])
+        nc.scalar.dma_start(g1[:], gate[0:P, CUT:SLOTS])
         load_a(0)
         load_w2(0)
         load_scales(w2_pl, w2_scales)
+        load_w2(1)
         for wt, ww in ((w1_t, w1_words), (w3_t, w3_words)):
             nc.sync.dma_start(wt[:].bitcast(I32), ww.bitcast(I32).rearrange("e s p c -> p (e s) c"))
         load_scales(w1_pl, w1_scales)
         load_scales(w3_pl, w3_scales)
-        load_w2(1)
         load_w2(2)
-        load_a(1)
         load_w2(3)
         pos_t = []
         for i, ps in enumerate((pos1, pos2)):
@@ -127,24 +128,30 @@ def tile_moe_bdx_glu_relu_kernel(
         gq, gs = {}, {}
         gf, gb, rm, dh, dag, dq, ds = {}, {}, {}, {}, {}, {}, {}
 
-        def gather(e, s, t, half):
-            lo, hi = (0, C) if half < 0 else (P * half, P * (half + 1))
-            if t == 0 and half <= 0:
-                g = work.tile([P, 4, C], F32, name="gf", bufs=5)
-                gf[e, s] = g
+        def gather(c, s, t, lo, hi):
+            base = 2 * P * 3 // 2 * c
+            if (c, s) not in gf:
+                g = work.tile([P, 4, CUT], F32, name="gf", bufs=4)
+                gf[c, s] = g
             nc.vector.tensor_tensor(
-                gf[e, s][:, t, lo:hi],
-                planes[4 * s + t][:].indirect(offs_t[:, (C * e + lo) // 16 : (C * e + hi) // 16]),
-                gates[e][:, lo:hi],
+                gf[c, s][:, t, lo - base : hi - base],
+                planes[4 * s + t][:].indirect(offs_t[:, lo // 16 : hi // 16]),
+                g0[:, lo:hi] if c == 0 else g1[:, lo - CUT : hi - CUT],
                 MULT,
             )
             if t == 3:
-                b = work.tile([P, C, 4], BF16, name="gb", bufs=5, align_bytes=64)
-                nc.scalar.copy(
-                    b[:, 0 : hi - lo, :].rearrange("p (c i) t -> p c t i", i=4),
-                    gf[e, s][:, :, lo:hi].rearrange("p t (c i) -> p c t i", i=4),
-                )
-                gb[C * e + lo, s] = b
+                at = lo
+                for a, b in PIECES:
+                    if a == at and b <= hi and (b == hi or b % C == 0):
+                        x = work.tile([P, C, 4], BF16, name="gb", bufs=7, align_bytes=64)
+                        nc.scalar.copy(
+                            x[:, 0 : b - a, :].rearrange("p (c i) t -> p c t i", i=4),
+                            gf[c, s][:, :, a - base : b - base].rearrange("p t (c i) -> p c t i", i=4),
+                        )
+                        gb[a, s] = x
+                        at = b
+                if (c, s) == (0, 2):
+                    load_a(1)
 
         def quantize(lo, hi, s):
             q = keep.tile([P, hi - lo], U32, name=f"gq{s}_{lo}", align_bytes=64)
@@ -166,7 +173,7 @@ def tile_moe_bdx_glu_relu_kernel(
                 nc.tensor.transpose(a1p[:, P * b : P * (b + 1)], a1_t[e][:, b, col : col + P], ident[:])
             for b in range(4):
                 nc.tensor.transpose(a3p[:, P * b : P * (b + 1)], a3_t[e][:, b, col : col + P], ident[:])
-            x = work.tile([P, 2, H], F32, name="rm", bufs=6)
+            x = work.tile([P, 2, H], F32, name="rm", bufs=5)
             nc.scalar.activation(x[:, 1, :], a1p[:], RELU)
             nc.vector.scalar_tensor_tensor(x[:, 0, :], x[:, 1, :], 0.0, a3p[:], IS_GT, MULT)
             rm[i] = x

from contextlib import ExitStack

import concourse.mybir as mybir
from concourse.masks import make_identity

K, T, E, C, H, N = 512, 512, 4, 256, 512, 1536
P = 128
S = N // 512
SLOTS = E * C
CUT = 384
PIECES = ((0, 256), (256, 384), (384, 512), (512, 768), (768, 896), (768, 1024), (896, 1024))

FLOPS = 2 * SLOTS * (N * H + 2 * H * K)
BYTES = 11210752

F32 = mybir.dt.float32
BF16 = mybir.dt.bfloat16
I32 = mybir.dt.int32
U32 = mybir.dt.uint32
U16 = mybir.dt.uint16
U8 = mybir.dt.uint8
FP8 = mybir.dt.float8_e4m3fn_x4
FP4 = mybir.dt.float4_e2m1fn_x4
MULT = mybir.AluOpType.mult
ADD = mybir.AluOpType.add
IS_GT = mybir.AluOpType.is_gt
RELU = mybir.ActivationFunctionType.Relu

PROGRAM = (
    ("g", 0, 0, 0, 0, 384), ("g", 0, 0, 1, 0, 384), ("g", 0, 0, 2, 0, 384), ("g", 0, 0, 3, 0, 384),
    ("m", 0), ("g", 0, 1, 0, 0, 384), ("g", 0, 1, 1, 0, 384), ("g", 0, 1, 2, 0, 384),
    ("g", 0, 1, 3, 0, 384), ("g", 0, 2, 0, 0, 384), ("g", 0, 2, 1, 0, 384), ("g", 0, 2, 2, 0, 384),
    ("m", 1), ("g", 0, 2, 3, 0, 384), ("g", 1, 0, 0, 384, 768), ("q", 256, 384, 0),
    ("q", 256, 384, 1), ("g", 1, 0, 1, 384, 768), ("q", 0, 256, 1), ("g", 1, 0, 2, 384, 768),
    ("q", 0, 256, 2), ("q", 256, 384, 2), ("q", 0, 256, 0), ("g", 1, 0, 3, 384, 768),
    ("g", 1, 1, 0, 384, 768), ("m", 2), ("q", 384, 512, 0), ("g", 1, 1, 1, 384, 768),
    ("g", 1, 1, 2, 384, 768), ("g", 1, 1, 3, 384, 768), ("dh", 0), ("da", 0),
    ("g", 1, 2, 0, 384, 768), ("g", 1, 2, 1, 384, 768), ("q", 384, 512, 1), ("g", 1, 2, 2, 384, 768),
    ("g", 1, 2, 3, 384, 768), ("dh", 1), ("dh", 2), ("da", 1),
    ("dq", 0), ("g", 2, 0, 0, 768, 1024), ("m", 3), ("q", 384, 512, 2),
    ("q", 512, 768, 0), ("g", 2, 0, 1, 768, 1024), ("dh", 3), ("da", 2),
    ("g", 2, 0, 2, 768, 1024), ("g", 2, 0, 3, 768, 1024), ("g", 2, 1, 0, 768, 1024), ("m", 4),
    ("da", 3), ("g", 2, 1, 1, 768, 1024), ("g", 2, 1, 2, 768, 1024), ("q", 512, 768, 1),
    ("m", 5), ("g", 2, 1, 3, 768, 1024), ("q", 512, 768, 2), ("g", 2, 2, 0, 768, 896),
    ("g", 2, 2, 1, 768, 896), ("dq", 1), ("g", 2, 2, 2, 768, 896), ("dh", 4),
    ("dq", 2), ("dh", 5), ("g", 2, 2, 3, 768, 896), ("m", 6),
    ("da", 4), ("q", 768, 1024, 0), ("da", 5), ("q", 768, 1024, 1),
    ("g", 2, 2, 0, 896, 1024), ("g", 2, 2, 1, 896, 1024), ("g", 2, 2, 2, 896, 1024), ("g", 2, 2, 3, 896, 1024),
    ("q", 768, 896, 2), ("dq", 3), ("dh", 6), ("q", 896, 1024, 2),
    ("m", 7), ("dh", 7), ("dq", 4), ("da", 6),
    ("da", 7), ("dq", 5), ("dq", 6), ("dq", 7),
)


def tile_moe_bdx_glu_relu_kernel(
    tc, dyT, a1, a3, w2_words, w2_scales, w1_words, w1_scales, w3_words, w3_scales, gate, offs, pos1, pos2, out
):
    nc = tc.nc
    with ExitStack() as ctx:
        keep = ctx.enter_context(tc.tile_pool(name="keep", bufs=1))
        work = ctx.enter_context(tc.tile_pool(name="work", bufs=3))
        psum = ctx.enter_context(tc.psum_pool(name="psum", bufs=1))

        offs_t = keep.tile([P, SLOTS // 16], U16, name="offs_t")
        nc.sync.dma_start(offs_t[:], offs)

        w2_pl = keep.tile([P, E * S, H], U8, name="w2_pl", align_bytes=64)
        w1_pl = keep.tile([P, E, K], U8, name="w1_pl", align_bytes=64)
        w3_pl = keep.tile([P, E, K], U8, name="w3_pl", align_bytes=64)
        for pl in (w2_pl, w1_pl, w3_pl):
            nc.vector.memset(pl[:].rearrange("p a b -> p (a b)").bitcast(I32), 0)
        ident = keep.tile([P, P], F32, name="ident")
        make_identity(nc, ident[:])

        gates, planes, w2_t, a1_t, a3_t = [], [], [], [], []
        dy_v = dyT.rearrange("(s p t) c -> s t p c", p=P, t=4)
        g0 = keep.tile([P, CUT], F32, name="gate_a")
        g1 = keep.tile([P, SLOTS - CUT], F32, name="gate_b")
        for i in range(S * 4):
            pt = keep.tile([P, T], F32, name=f"plane{i}")
            planes.append(pt)
        for e in range(E):
            w = keep.tile([P, S, 2 * H], U8, name=f"w2_{e}", align_bytes=64)
            w2_t.append(w)
        w1_t = keep.tile([P, E, 2 * K], U8, name="w1_t", align_bytes=64)
        w3_t = keep.tile([P, E, 2 * K], U8, name="w3_t", align_bytes=64)
        for e in range(2):
            x1 = keep.tile([P, 4, 2 * C], F32, name=f"a1_{e}")
            x3 = keep.tile([P, 4, 2 * C], F32, name=f"a3_{e}")
            a1_t.append(x1)
            a3_t.append(x3)

        def load_w2(e):
            nc.sync.dma_start(w2_t[e][:].bitcast(I32), w2_words[e].bitcast(I32).rearrange("s p c -> p s c"))

        def load_a(e):
            nc.scalar.dma_start(a1_t[e][:], a1.rearrange("(b p) j -> p b j", p=P)[:, :, 2 * C * e : 2 * C * (e + 1)])
            nc.scalar.dma_start(a3_t[e][:], a3.rearrange("(b p) j -> p b j", p=P)[:, :, 2 * C * e : 2 * C * (e + 1)])

        def load_scales(pl, sc):
            for q in range(4):
                nc.sync.dma_start(
                    pl[32 * q : 32 * q + 4].bitcast(I32),
                    sc.bitcast(I32).rearrange("e s f i -> f (e s) i")[4 * q : 4 * q + 4],
                )

        nc.scalar.dma_start(g0[:], gate[0:P, 0:CUT])
        for i in range(S * 4):
            (nc.scalar if i % 2 else nc.sync).dma_start(planes[i][:], dy_v[i // 4, i % 4])
        nc.scalar.dma_start(g1[:], gate[0:P, CUT:SLOTS])
        load_a(0)
        load_w2(0)
        load_scales(w2_pl, w2_scales)
        load_w2(1)
        for wt, ww in ((w1_t, w1_words), (w3_t, w3_words)):
            nc.sync.dma_start(wt[:].bitcast(I32), ww.bitcast(I32).rearrange("e s p c -> p (e s) c"))
        load_scales(w1_pl, w1_scales)
        load_scales(w3_pl, w3_scales)
        load_w2(2)
        load_w2(3)
        pos_t = []
        for i, ps in enumerate((pos1, pos2)):
            pp = keep.tile([P, T // 16], U16, name=f"pos_t{i}")
            nc.sync.dma_start(pp[:], ps)
            pos_t.append(pp)

        dx = keep.tile([P, 4, SLOTS], F32, name="dx")
        gq, gs = {}, {}
        gf, gb, rm, dh, dag, dq, ds = {}, {}, {}, {}, {}, {}, {}

        def gather(c, s, t, lo, hi):
            base = 2 * P * 3 // 2 * c
            if (c, s) not in gf:
                g = work.tile([P, 4, CUT], F32, name="gf", bufs=4)
                gf[c, s] = g
            nc.vector.tensor_tensor(
                gf[c, s][:, t, lo - base : hi - base],
                planes[4 * s + t][:].indirect(offs_t[:, lo // 16 : hi // 16]),
                g0[:, lo:hi] if c == 0 else g1[:, lo - CUT : hi - CUT],
                MULT,
            )
            if t == 3:
                at = lo
                for a, b in PIECES:
                    if a == at and b <= hi and (b == hi or b % C == 0):
                        x = work.tile([P, C, 4], BF16, name="gb", bufs=7, align_bytes=64)
                        nc.scalar.copy(
                            x[:, 0 : b - a, :].rearrange("p (c i) t -> p c t i", i=4),
                            gf[c, s][:, :, a - base : b - base].rearrange("p t (c i) -> p c t i", i=4),
                        )
                        gb[a, s] = x
                        at = b
                if (c, s) == (0, 2):
                    load_a(1)

        def quantize(lo, hi, s):
            q = keep.tile([P, hi - lo], U32, name=f"gq{s}_{lo}", align_bytes=64)
            z = keep.tile([P, hi - lo], U8, name=f"gs{s}_{lo}", align_bytes=64)
            for i in range(lo // P, hi // P):
                gq[i, s] = q[:, P * i - lo : P * i - lo + P]
                gs[i, s] = z[:, P * i - lo : P * i - lo + P]
            nc.vector.quantize_mx(
                out=q[:].bitcast(FP8),
                scales=z[:],
                in_=gb[lo, s][:, 0 : hi - lo, :].rearrange("p c t -> p (c t)"),
            )

        def saved(i):
            e, col = i // 4, P * (i % 4)
            a1p = psum.tile([P, H], F32, name="a1p", bufs=1)
            a3p = psum.tile([P, H], F32, name="a3p", bufs=1)
            for b in range(4):
                nc.tensor.transpose(a1p[:, P * b : P * (b + 1)], a1_t[e][:, b, col : col + P], ident[:])
            for b in range(4):
                nc.tensor.transpose(a3p[:, P * b : P * (b + 1)], a3_t[e][:, b, col : col + P], ident[:])
            x = work.tile([P, 2, H], F32, name="rm", bufs=5)
            nc.scalar.activation(x[:, 1, :], a1p[:], RELU)
            nc.vector.scalar_tensor_tensor(x[:, 0, :], x[:, 1, :], 0.0, a3p[:], IS_GT, MULT)
            rm[i] = x

        def first(i):
            e = i // 2
            acc = psum.tile([P, H], F32, name="dh", bufs=2)
            for s in range(S):
                nc.tensor.matmul_mx(
                    out=acc[:],
                    lhsT=gq[i, s].bitcast(FP8),
                    lhsT_scale=gs[i, s],
                    rhs=w2_t[e][:, s, :].bitcast(FP4),
                    rhs_scale=w2_pl[:, S * e + s, :],
                    start=(s == 0),
                    stop=(s == S - 1),
                )
            dh[i] = acc

        def grads(i):
            last = i == 7
            da = work.tile([P, 2, H], BF16, name="da", bufs=3, align_bytes=64)
            if last:
                for w in range(2):
                    nc.vector.tensor_tensor(da[:, w, :], dh[i][:], rm[i][:, w, :], MULT)
            else:
                nc.vector.tensor_tensor(da[:], dh[i][:].unsqueeze(1).to_broadcast([P, 2, H]), rm[i][:], MULT)
            dap = psum.tile([P, 2, 2, P], F32, name="dap", bufs=2)
            for w in range(2):
                words = da[:, w, :].bitcast(F32)
                for u in range(2):
                    nc.tensor.transpose(dap[:, w, u, :], words[:, u:256:2], ident[:])
            g = work.tile([P, 2 * P * 4], BF16, name="dag", bufs=3, align_bytes=64)
            g_v = g[:].bitcast(F32).rearrange("p (w r u) -> p w r u", w=2, u=2)
            dap_v = dap[:].rearrange("p w u r -> p w r u")
            if last:
                for w in range(2):
                    nc.scalar.copy(g_v[:, w], dap_v[:, w])
            else:
                nc.scalar.copy(g_v, dap_v)
            dag[i] = g

        def second(i):
            last = i == 7
            q = work.tile([P, 2 * P], U32, name="dq", bufs=3, align_bytes=64)
            z = work.tile([P, 2 * P], U8, name="ds", bufs=3, align_bytes=64)
            for a, b in ((0, P), (P, 2 * P)) if last else ((0, 2 * P),):
                nc.vector.quantize_mx(out=q[:, a:b].bitcast(FP8), scales=z[:, a:b], in_=dag[i][:, 4 * a : 4 * b])
            dxp = psum.tile([P, 4, P], F32, name="dxp", bufs=2)
            j0 = P * i
            for kt in range(4):
                for w, (wt, pl) in enumerate(((w1_t, w1_pl), (w3_t, w3_pl))):
                    nc.tensor.matmul_mx(
                        out=dxp[:, kt, :],
                        lhsT=wt[:, i // 2, 256 * kt : 256 * (kt + 1)].bitcast(FP4),
                        lhsT_scale=pl[:, i // 2, P * kt : P * (kt + 1)],
                        rhs=q[:, P * w : P * (w + 1)].bitcast(FP8),
                        rhs_scale=z[:, P * w : P * (w + 1)],
                        start=(w == 0),
                        stop=(w == 1),
                    )
                if last:
                    nc.scalar.copy(dx[:, kt, j0 : j0 + P], dxp[:, kt, :])
            if not last:
                nc.scalar.copy(dx[:, :, j0 : j0 + P], dxp[:])

        steps = {"g": gather, "q": quantize, "m": saved, "dh": first, "da": grads, "dq": second}
        for step in PROGRAM:
            steps[step[0]](*step[1:])

        for kt in range(4):
            o1 = work.tile([P, T], F32, name="o1", bufs=2)
            o2 = work.tile([P, T], F32, name="o2", bufs=2)
            o = work.tile([P, T], F32, name="o", bufs=2)
            nc.vector.tensor_copy(o1[:], dx[:, kt, :].indirect(pos_t[0][:]))
            nc.vector.tensor_copy(o2[:], dx[:, kt, :].indirect(pos_t[1][:]))
            (nc.vector if kt == 3 else nc.gpsimd).tensor_tensor(o[:], o1[:], o2[:], ADD)
            nc.sync.dma_start(out[P * kt : P * (kt + 1), :], o[:])
